import numpy as np
import ml_dtypes


def mxq(x, axis, fmt="e4m3"):
    dtype, down = {"e4m3": (ml_dtypes.float8_e4m3fn, 7), "e5m2": (ml_dtypes.float8_e5m2, 14)}[fmt]
    v = np.moveaxis(np.asarray(x, np.float32).astype(ml_dtypes.bfloat16).astype(np.float64), axis, -1)
    blocks = v.reshape(v.shape[:-1] + (-1, 32))
    amax = np.abs(blocks).max(-1, keepdims=True)
    byte = np.maximum(np.where(amax > 0, np.frexp(amax)[1] - 1 + 127, 0) - down, 1)
    scale = np.exp2(byte - 127.0)
    codes = (blocks / scale).astype(np.float32).astype(dtype).astype(np.float64)
    return np.moveaxis((codes * scale).reshape(v.shape), -1, axis)


WIDE = False


def mx_kscale(k):
    if not WIDE:
        return np.ones(k)
    levels = np.array([10, -10, 5, -5, 0])
    if k % 512:
        return np.exp2(np.random.permutation(np.resize(levels, k // 32))).repeat(32)
    a = np.empty((k // 512, 16))
    for p in range(k // 512):
        a[p, :8] = np.random.permutation(np.resize(levels, 8))
        for g in range(8):
            far = levels[np.abs(levels - a[p, g]) >= 10]
            a[p, g + 8] = far[np.random.randint(len(far))]
    return np.exp2(a.ravel()).repeat(32)


def f64(x):
    return np.asarray(x).astype(np.float64)


def striped(idx):
    return np.tile(np.asarray(idx).reshape(-1, 16).T, (8, 1)).astype(np.uint16)


def unstriped(offs):
    return offs[:16].T.reshape(-1).astype(np.int64)


E2M1 = np.array([0.0, 0.5, 1.0, 1.5, 2.0, 3.0, 4.0, 6.0, -0.0, -0.5, -1.0, -1.5, -2.0, -3.0, -4.0, -6.0])


def pack_weight(w, fmt):
    k, n = w.shape
    w = f64(np.asarray(w, np.float32).astype(ml_dtypes.bfloat16)).reshape(k // 32, 32, n)
    amax = np.abs(w).max(1)
    if fmt == "e4m3":
        byte = np.frexp(amax)[1] - 1 + 127 - 7
    else:
        mant, ex = np.frexp(amax / 6.0)
        byte = np.where(mant > 0.5, ex, ex - 1) + 127
    byte = np.clip(np.where(amax > 0, byte, 1), 1, 254)
    scaled = (w * np.exp2(127.0 - byte)[:, None, :]).reshape(k, n).astype(np.float32)
    by_word = np.ascontiguousarray(scaled.reshape(k // 512, 128, 4, n).transpose(0, 1, 3, 2))
    if fmt == "e4m3":
        words = by_word.astype(ml_dtypes.float8_e4m3fn).view(np.uint8)
    else:
        c = by_word.astype(ml_dtypes.float4_e2m1fn).view(np.uint8) & 0xF
        words = (c[..., 0::2] | (c[..., 1::2] << 4)).reshape(k // 512, 128, 2 * n)
    return np.ascontiguousarray(words), np.ascontiguousarray(byte.astype(np.uint8).reshape(k // 512, 16, n))


def unpack_weight(words, scales, fmt):
    g, _, n = scales.shape
    words = np.ascontiguousarray(words).reshape(g, 128, n, -1)
    if fmt == "e4m3":
        vals = words.view(ml_dtypes.float8_e4m3fn).astype(np.float64)
    else:
        nib = np.empty((g, 128, n, 4), np.uint8)
        nib[..., 0::2] = words & 0xF
        nib[..., 1::2] = words >> 4
        vals = E2M1[nib]
    vals = vals * np.repeat(np.exp2(scales.astype(np.float64) - 127.0), 8, axis=1)[..., None]
    return vals.transpose(0, 1, 3, 2).reshape(g * 512, n)


D, T, I, Q, E, K = 512, 1024, 512, 128, 512, 1024


def setup_inputs():
    n = np.random.standard_normal
    idx = np.random.permutation(T)[:I]
    fd = mx_kscale(D)
    fk = mx_kscale(K)
    fi = mx_kscale(I)
    ti = np.ones(T)
    ti[idx] = fi
    krestp = pack_weight(n((K, T)) / fk[:, None], "e4m3")
    return {
        "query": (n((D, Q)) * 0.2 / np.sqrt(D) * fd[:, None]).astype(np.float32),
        "kfirst": (n((D, T)) / fd[:, None]).astype(np.float32),
        "qrest": (n((K, Q)) * 0.2 / np.sqrt(K) * fk[:, None]).astype(np.float32),
        "krest_words": krestp[0],
        "krest_scales": krestp[1],
        "size": (np.random.uniform(0.5, 2.0, (1, I)) * fi).astype(np.float32),
        "vals": (n((E, T)) / ti).astype(np.float32),
        "offs": striped(idx),
    }


def reference(query, kfirst, qrest, krest_words, krest_scales, size, vals, offs):
    idx = unstriped(offs)
    krestu = unpack_weight(krest_words, krest_scales, "e4m3")
    queryq = mxq(f64(query), 0, "e4m3")
    kfirstq = mxq(f64(kfirst), 0, "e4m3")
    a = queryq.T @ kfirstq
    qrestq = mxq(f64(qrest), 0, "e4m3")
    krestidxg = krestu[:, idx]
    b = qrestq.T @ krestidxg
    s = a[:, idx] + b
    p = np.exp(s - np.max(s, axis=1, keepdims=True))
    w = p * f64(size) / np.sum(p, axis=1, keepdims=True)
    wt = w.T
    vt = f64(vals)[:, idx].T
    wtq = mxq(wt, 0, "e4m3")
    vtq = mxq(vt, 0, "e4m3")
    o = wtq.T @ vtq
    return o

@@ -1,0 +1,224 @@
+from contextlib import ExitStack
+
+import concourse.mybir as mybir
+from concourse.masks import make_identity
+
+D, T, I, Q, E, K = 512, 1024, 512, 128, 512, 1024
+FLOPS = 2 * Q * (D * T + K * I + I * E)
+
+F32 = mybir.dt.float32
+BF16 = mybir.dt.bfloat16
+I32 = mybir.dt.int32
+U32 = mybir.dt.uint32
+U16 = mybir.dt.uint16
+U8 = mybir.dt.uint8
+FP8X4 = mybir.dt.float8_e4m3fn_x4
+ALU = mybir.AluOpType
+ACT = mybir.ActivationFunctionType
+AX = mybir.AxisListType
+
+P = 128
+PACK = 4
+PASS = P * PACK
+CHUNK = 256
+K_SPLIT = 128
+
+
+def tile_attend_prefixfeatures_kernel(tc, query, kfirst, qrest, krest_words, krest_scales, size, vals, offs, out):
+    nc = tc.nc
+    with ExitStack() as ctx:
+        sb = ctx.enter_context(tc.tile_pool(name="sb", bufs=1))
+        ps = ctx.enter_context(tc.psum_pool(name="ps", bufs=1))
+
+        def bank(n, shape):
+            return ps.tile(shape, F32, name="bank%d" % n, tag="bank%d" % n)
+
+        def interleave(engine_copy, raw, width, name):
+            grouped = sb.tile([P, width, PACK], BF16, name=name, align_bytes=64)
+            engine_copy(
+                grouped[:].rearrange("p (c i) t -> p c t i", i=4),
+                raw[:].rearrange("p t (c i) -> p c t i", i=4),
+            )
+            return grouped
+
+        def quantize(grouped, width, name):
+            codes = sb.tile([P, width], U32, name=name + "_codes", align_bytes=64)
+            scales = sb.tile([P, width], U8, name=name + "_scales", align_bytes=64)
+            nc.vector.quantize_mx(
+                out=codes[:].bitcast(FP8X4), scales=scales[:], in_=grouped[:].rearrange("p c t -> p (c t)")
+            )
+            return codes, scales
+
+        def product(acc, stationary, moving, start, stop):
+            nc.tensor.matmul_mx(
+                out=acc,
+                lhsT=stationary[0].bitcast(FP8X4),
+                lhsT_scale=stationary[1],
+                rhs=moving[0].bitcast(FP8X4),
+                rhs_scale=moving[1],
+                start=start,
+                stop=stop,
+            )
+
+        offsets = sb.tile([P, I // 16], U16, name="offsets")
+        nc.sync.dma_start(offsets[:], offs)
+
+        scale_pool = sb.tile([P, T], U8, name="scale_pool", align_bytes=64)
+        nc.vector.memset(scale_pool[:].bitcast(I32), 0)
+        for quad in range(4):
+            nc.scalar.dma_start(
+                scale_pool[32 * quad : 32 * quad + 8, :].bitcast(I32),
+                krest_scales[:, 4 * quad : 4 * quad + 4, :].bitcast(I32),
+            )
+        warm = sb.tile([P, 1], F32, name="warm")
+        nc.vector.memset(warm[:], 0.0)
+        warm_out = sb.tile([P, 1], F32, name="warm_out")
+        nc.scalar.activation(warm_out[:], warm[:], ACT.Exp)
+
+        query_raw = sb.tile([P, PACK, Q], F32, name="query_raw")
+
+        kview = kfirst.rearrange("(p t) n -> p t n", t=PACK)
+        k_raw = [sb.tile([P, PACK, CHUNK], F32, name="k_raw%d" % c) for c in range(T // CHUNK)]
+        word_pool = [sb.tile([P, T], U32, name="word_pool%d" % z) for z in range(2)]
+        qrest_raw = [sb.tile([P, PACK, Q], F32, name="qrest_raw%d" % z) for z in range(2)]
+        val_pool = [sb.tile([P, T], F32, name="val_pool%d" % c, tag="val_pool%d" % c) for c in range(E // P)]
+        size_cols = sb.tile([P, PACK], F32, name="size_cols")
+
+        def load_k(c):
+            nc.sync.dma_start(k_raw[c][:], kview[:, :, c * CHUNK : (c + 1) * CHUNK])
+
+        def load_words(z):
+            nc.sync.dma_start(word_pool[z][:].bitcast(I32), krest_words[z].rearrange("p n t -> p (n t)").bitcast(I32))
+
+        load_words(0)
+        load_words(1)
+        nc.sync.dma_start(query_raw[:], query.rearrange("(p t) q -> p t q", t=PACK))
+        for c in range(T // CHUNK):
+            load_k(c)
+        for z in range(2):
+            nc.sync.dma_start(qrest_raw[z][:], qrest[z * PASS : (z + 1) * PASS, :].rearrange("(p t) q -> p t q", t=PACK))
+        nc.scalar.dma_start(size_cols[:], size.rearrange("o (p t) -> (o p) t", t=PACK))
+        for c in range(E // P):
+            nc.sync.dma_start(val_pool[c][:], vals[c * P : (c + 1) * P, :])
+
+        ident = sb.tile([P, P], F32, name="ident")
+        make_identity(nc, ident[:])
+
+        scale_listed = sb.tile([P, I], U8, name="scale_listed", align_bytes=64)
+        nc.vector.tensor_copy(scale_listed[:], scale_pool[:].indirect(offsets[:]))
+
+
+        size_rows = bank(7, [P, PACK, P])
+        for t in range(PACK):
+            nc.tensor.transpose(size_rows[:, t, :], size_cols[:, t : t + 1].to_broadcast([P, P]), ident[:])
+
+        a_all = sb.tile([P, T], F32, name="a_all")
+        words_listed = [sb.tile([P, I], U32, name="words_listed%d" % z, align_bytes=64) for z in range(2)]
+
+        def prefix_scores(c):
+            grouped = sb.tile([P, CHUNK, PACK], BF16, name="k_g%d" % c, align_bytes=64)
+            for engine_copy, cols in ((nc.vector.tensor_copy, slice(0, K_SPLIT)), (nc.scalar.copy, slice(K_SPLIT, CHUNK))):
+                engine_copy(
+                    grouped[:, cols, :].rearrange("p (c i) t -> p c t i", i=4),
+                    k_raw[c][:, :, cols].rearrange("p t (c i) -> p c t i", i=4),
+                )
+            k_mx = quantize(grouped, CHUNK, "k%d" % c)
+            acc = bank(c, [P, CHUNK])
+            product(acc[:], query_op, (k_mx[0][:], k_mx[1][:]), True, True)
+            nc.scalar.copy(a_all[:, c * CHUNK : (c + 1) * CHUNK], acc[:])
+
+        def gather_words(z):
+            nc.vector.tensor_copy(words_listed[z][:], word_pool[z][:].indirect(offsets[:]))
+
+        gather_words(0)
+        gather_words(1)
+        query_mx = quantize(interleave(nc.scalar.copy, query_raw, Q, "query_g"), Q, "query")
+        query_op = (query_mx[0][:], query_mx[1][:])
+        for c in range(T // CHUNK):
+            prefix_scores(c)
+
+        b_acc = bank(4, [P, I])
+
+        def rest_scores(z, engine_copy):
+            q_mx = quantize(interleave(engine_copy, qrest_raw[z], Q, "qrest_g%d" % z), Q, "qrest%d" % z)
+            product(
+                b_acc[:], (q_mx[0][:], q_mx[1][:]), (words_listed[z][:], scale_listed[4 * z : P, :]), z == 0, z == 1
+            )
+
+        rest_scores(0, nc.vector.tensor_copy)
+        a_listed = sb.tile([P, I], F32, name="a_listed")
+        nc.vector.tensor_copy(a_listed[:], a_all[:].indirect(offsets[:]))
+        rest_scores(1, nc.scalar.copy)
+
+        val_half = sb.tile([P, T], BF16, name="val_half")
+        nc.scalar.activation(val_half[:], val_pool[0][:], ACT.Copy)
+
+        s = sb.tile([P, I], F32, name="s", tag="s", align_bytes=64)
+        nc.vector.tensor_tensor(s[:], a_listed[:], b_acc[:], ALU.add)
+        neg_max = sb.tile([P, 1], F32, name="neg_max")
+        nc.vector.tensor_reduce(neg_max[:], s[:], AX.X, ALU.max, negate=True)
+        p = sb.tile([P, I], F32, name="p", tag="val_pool0")
+        row_sum = sb.tile([P, 1], F32, name="row_sum")
+        nc.scalar.activation(p[:], s[:], ACT.Exp, bias=neg_max[:], scale=1.0, accum_out=row_sum[:])
+
+        def turn(src, n, name):
+            words = src[:].bitcast(F32)
+            turned = bank(n, [P, 2, P])
+            for u in range(2):
+                nc.tensor.transpose(turned[:, u, :], words[:, u : I // 2 : 2], ident[:])
+            grouped = sb.tile([P, P, PACK], BF16, name=name, align_bytes=64)
+            nc.scalar.copy(
+                grouped[:].rearrange("p c t -> p (c t)").bitcast(F32).rearrange("p (c u) -> p c u", u=2),
+                turned[:].rearrange("p u c -> p c u"),
+            )
+            return grouped
+
+        v_codes = sb.tile([P, E], U32, name="v_codes", align_bytes=64)
+        v_scales = sb.tile([P, E], U8, name="v_scales", align_bytes=64)
+
+        def gather_values(c):
+            listed = sb.tile([P, I], BF16, name="val_listed%d" % c, align_bytes=64)
+            nc.vector.tensor_copy(listed[:], val_pool[c][:].indirect(offsets[:]))
+            return turn(listed, c, "v_g%d" % c)
+
+        def quantize_values(c, grouped):
+            cols = slice(c * P, (c + 1) * P)
+            nc.vector.quantize_mx(
+                out=v_codes[:, cols].bitcast(FP8X4), scales=v_scales[:, cols], in_=grouped[:].rearrange("p c t -> p (c t)")
+            )
+
+        v1 = gather_values(1)
+        inv_sum = sb.tile([P, 1], F32, name="inv_sum")
+        nc.vector.reciprocal(inv_sum[:], row_sum[:])
+        w = sb.tile([P, I], BF16, name="w", align_bytes=64)
+        nc.vector.scalar_tensor_tensor(
+            w[:].rearrange("q (p t) -> q p t", t=PACK),
+            p[:].rearrange("q (p t) -> q p t", t=PACK),
+            inv_sum[:],
+            size_rows[:].rearrange("q t p -> q p t"),
+            ALU.mult,
+            ALU.mult,
+        )
+        listed0 = sb.tile([P, I], BF16, name="val_listed0", tag="s", align_bytes=64)
+        nc.scalar.activation(listed0[:], val_half[:].indirect(offsets[:]), ACT.Copy)
+        w_g = turn(w, 4, "w_g")
+        v0 = turn(listed0, 0, "v_g0")
+        v2 = gather_values(2)
+        quantize_values(1, v1)
+        w_mx = quantize(w_g, Q, "w")
+        w_op = (w_mx[0][:], w_mx[1][:])
+        quantize_values(0, v0)
+
+        def finish(n, lo, hi, engine_copy, name):
+            acc = bank(n, [P, hi - lo])
+            product(acc[:], w_op, (v_codes[:, lo:hi], v_scales[:, lo:hi]), True, True)
+            res = sb.tile([P, hi - lo], F32, name=name)
+            engine_copy(res[:], acc[:])
+            nc.sync.dma_start(out[:, lo:hi], res[:])
+
+        finish(5, 0, 2 * P, nc.scalar.copy, "res0")
+        v3 = gather_values(3)
+        quantize_values(2, v2)
+        finish(6, 2 * P, 3 * P, nc.scalar.copy, "res1")
+        quantize_values(3, v3)
+        finish(4, 3 * P, 4 * P, nc.scalar.copy, "res2")

@@ -1,7 +1,6 @@
 from contextlib import ExitStack
 
 import concourse.mybir as mybir
-from concourse.masks import make_identity
 
 D, T, I, Q, E, K = 512, 1024, 512, 128, 512, 1024
 FLOPS = 2 * Q * (D * T + K * I + I * E)
@@ -21,7 +20,8 @@ P = 128
 PACK = 4
 PASS = P * PACK
 CHUNK = 256
-K_SPLIT = 128
+K_LOADS = (512, 256, 256)
+VECTOR_SHARE = (160, 160, 64, 128)
 
 
 def tile_attend_prefixfeatures_kernel(tc, query, kfirst, qrest, krest_words, krest_scales, size, vals, offs, out):
@@ -30,26 +30,30 @@ def tile_attend_prefixfeatures_kernel(tc, query, kfirst, qrest, krest_words, kre
         sb = ctx.enter_context(tc.tile_pool(name="sb", bufs=1))
         ps = ctx.enter_context(tc.psum_pool(name="ps", bufs=1))
 
+        def tile(shape, dtype, name, after=None):
+            return sb.tile(shape, dtype, name=name, tag=after or name, align_bytes=64)
+
+        def ring_tile(shape, name):
+            return sb.tile(shape, BF16, name=name, tag="ring", bufs=2, align_bytes=64)
+
         def bank(n, shape):
             return ps.tile(shape, F32, name="bank%d" % n, tag="bank%d" % n)
 
-        def interleave(engine_copy, raw, width, name):
-            grouped = sb.tile([P, width, PACK], BF16, name=name, align_bytes=64)
-            engine_copy(
-                grouped[:].rearrange("p (c i) t -> p c t i", i=4),
-                raw[:].rearrange("p t (c i) -> p c t i", i=4),
-            )
-            return grouped
+        def interleave(engine_copy, grouped, raw):
+            engine_copy(grouped.rearrange("p (c i) t -> p c t i", i=4), raw.rearrange("p t (c i) -> p c t i", i=4))
 
-        def quantize(grouped, width, name):
-            codes = sb.tile([P, width], U32, name=name + "_codes", align_bytes=64)
-            scales = sb.tile([P, width], U8, name=name + "_scales", align_bytes=64)
+        def mx_tiles(width, name, after=None):
+            return tile([P, width], U32, name + "_codes", after), tile([P, width], U8, name + "_scales")
+
+        def columns(operand, lo, hi):
+            return operand[0][:, lo:hi], operand[1][:, lo:hi]
+
+        def quantize(operand, grouped):
             nc.vector.quantize_mx(
-                out=codes[:].bitcast(FP8X4), scales=scales[:], in_=grouped[:].rearrange("p c t -> p (c t)")
+                out=operand[0].bitcast(FP8X4), scales=operand[1], in_=grouped.rearrange("p c t -> p (c t)")
             )
-            return codes, scales
 
-        def product(acc, stationary, moving, start, stop):
+        def product(acc, stationary, moving, start=True, stop=True):
             nc.tensor.matmul_mx(
                 out=acc,
                 lhsT=stationary[0].bitcast(FP8X4),
@@ -60,137 +64,140 @@ def tile_attend_prefixfeatures_kernel(tc, query, kfirst, qrest, krest_words, kre
                 stop=stop,
             )
 
-        offsets = sb.tile([P, I // 16], U16, name="offsets")
-        nc.sync.dma_start(offsets[:], offs)
+        def load_values(c, after=None):
+            pool = tile([P, T], F32, "val_pool%d" % c, after)
+            nc.sync.dma_start(pool[:], vals[c * P : (c + 1) * P, :])
+            return pool
 
-        scale_pool = sb.tile([P, T], U8, name="scale_pool", align_bytes=64)
-        nc.vector.memset(scale_pool[:].bitcast(I32), 0)
-        for quad in range(4):
-            nc.scalar.dma_start(
-                scale_pool[32 * quad : 32 * quad + 8, :].bitcast(I32),
-                krest_scales[:, 4 * quad : 4 * quad + 4, :].bitcast(I32),
-            )
-        warm = sb.tile([P, 1], F32, name="warm")
-        nc.vector.memset(warm[:], 0.0)
-        warm_out = sb.tile([P, 1], F32, name="warm_out")
-        nc.scalar.activation(warm_out[:], warm[:], ACT.Exp)
+        def gather_on_scalar(pool, name, after=None):
+            rounded = tile([P, T], BF16, name + "_rounded", after)
+            nc.scalar.activation(rounded[:], pool[:], ACT.Copy)
+            listed = tile([P, I], BF16, name)
+            nc.scalar.activation(listed[:], rounded[:].indirect(offsets[:]), ACT.Copy)
+            return listed
 
-        query_raw = sb.tile([P, PACK, Q], F32, name="query_raw")
+        def gather_on_vector(listed, pool):
+            nc.vector.tensor_copy(listed[:], pool[:].indirect(offsets[:]))
 
-        kview = kfirst.rearrange("(p t) n -> p t n", t=PACK)
-        k_raw = [sb.tile([P, PACK, CHUNK], F32, name="k_raw%d" % c) for c in range(T // CHUNK)]
-        word_pool = [sb.tile([P, T], U32, name="word_pool%d" % z) for z in range(2)]
-        qrest_raw = [sb.tile([P, PACK, Q], F32, name="qrest_raw%d" % z) for z in range(2)]
-        val_pool = [sb.tile([P, T], F32, name="val_pool%d" % c, tag="val_pool%d" % c) for c in range(E // P)]
-        size_cols = sb.tile([P, PACK], F32, name="size_cols")
-
-        def load_k(c):
-            nc.sync.dma_start(k_raw[c][:], kview[:, :, c * CHUNK : (c + 1) * CHUNK])
-
-        def load_words(z):
-            nc.sync.dma_start(word_pool[z][:].bitcast(I32), krest_words[z].rearrange("p n t -> p (n t)").bitcast(I32))
-
-        load_words(0)
-        load_words(1)
-        nc.sync.dma_start(query_raw[:], query.rearrange("(p t) q -> p t q", t=PACK))
-        for c in range(T // CHUNK):
-            load_k(c)
-        for z in range(2):
-            nc.sync.dma_start(qrest_raw[z][:], qrest[z * PASS : (z + 1) * PASS, :].rearrange("(p t) q -> p t q", t=PACK))
-        nc.scalar.dma_start(size_cols[:], size.rearrange("o (p t) -> (o p) t", t=PACK))
-        for c in range(E // P):
-            nc.sync.dma_start(val_pool[c][:], vals[c * P : (c + 1) * P, :])
-
-        ident = sb.tile([P, P], F32, name="ident")
-        make_identity(nc, ident[:])
-
-        scale_listed = sb.tile([P, I], U8, name="scale_listed", align_bytes=64)
-        nc.vector.tensor_copy(scale_listed[:], scale_pool[:].indirect(offsets[:]))
-
-
-        size_rows = bank(7, [P, PACK, P])
-        for t in range(PACK):
-            nc.tensor.transpose(size_rows[:, t, :], size_cols[:, t : t + 1].to_broadcast([P, P]), ident[:])
-
-        a_all = sb.tile([P, T], F32, name="a_all")
-        words_listed = [sb.tile([P, I], U32, name="words_listed%d" % z, align_bytes=64) for z in range(2)]
-
-        def prefix_scores(c):
-            grouped = sb.tile([P, CHUNK, PACK], BF16, name="k_g%d" % c, align_bytes=64)
-            for engine_copy, cols in ((nc.vector.tensor_copy, slice(0, K_SPLIT)), (nc.scalar.copy, slice(K_SPLIT, CHUNK))):
-                engine_copy(
-                    grouped[:, cols, :].rearrange("p (c i) t -> p c t i", i=4),
-                    k_raw[c][:, :, cols].rearrange("p t (c i) -> p c t i", i=4),
-                )
-            k_mx = quantize(grouped, CHUNK, "k%d" % c)
-            acc = bank(c, [P, CHUNK])
-            product(acc[:], query_op, (k_mx[0][:], k_mx[1][:]), True, True)
-            nc.scalar.copy(a_all[:, c * CHUNK : (c + 1) * CHUNK], acc[:])
-
-        def gather_words(z):
-            nc.vector.tensor_copy(words_listed[z][:], word_pool[z][:].indirect(offsets[:]))
-
-        gather_words(0)
-        gather_words(1)
-        query_mx = quantize(interleave(nc.scalar.copy, query_raw, Q, "query_g"), Q, "query")
-        query_op = (query_mx[0][:], query_mx[1][:])
-        for c in range(T // CHUNK):
-            prefix_scores(c)
-
-        b_acc = bank(4, [P, I])
-
-        def rest_scores(z, engine_copy):
-            q_mx = quantize(interleave(engine_copy, qrest_raw[z], Q, "qrest_g%d" % z), Q, "qrest%d" % z)
-            product(
-                b_acc[:], (q_mx[0][:], q_mx[1][:]), (words_listed[z][:], scale_listed[4 * z : P, :]), z == 0, z == 1
-            )
-
-        rest_scores(0, nc.vector.tensor_copy)
-        a_listed = sb.tile([P, I], F32, name="a_listed")
-        nc.vector.tensor_copy(a_listed[:], a_all[:].indirect(offsets[:]))
-        rest_scores(1, nc.scalar.copy)
-
-        val_half = sb.tile([P, T], BF16, name="val_half")
-        nc.scalar.activation(val_half[:], val_pool[0][:], ACT.Copy)
-
-        s = sb.tile([P, I], F32, name="s", tag="s", align_bytes=64)
-        nc.vector.tensor_tensor(s[:], a_listed[:], b_acc[:], ALU.add)
-        neg_max = sb.tile([P, 1], F32, name="neg_max")
-        nc.vector.tensor_reduce(neg_max[:], s[:], AX.X, ALU.max, negate=True)
-        p = sb.tile([P, I], F32, name="p", tag="val_pool0")
-        row_sum = sb.tile([P, 1], F32, name="row_sum")
-        nc.scalar.activation(p[:], s[:], ACT.Exp, bias=neg_max[:], scale=1.0, accum_out=row_sum[:])
-
-        def turn(src, n, name):
+        def turn(src, n, name, after=None):
             words = src[:].bitcast(F32)
             turned = bank(n, [P, 2, P])
             for u in range(2):
                 nc.tensor.transpose(turned[:, u, :], words[:, u : I // 2 : 2], ident[:])
-            grouped = sb.tile([P, P, PACK], BF16, name=name, align_bytes=64)
+            grouped = tile([P, P, PACK], BF16, name, after)
             nc.scalar.copy(
                 grouped[:].rearrange("p c t -> p (c t)").bitcast(F32).rearrange("p (c u) -> p c u", u=2),
                 turned[:].rearrange("p u c -> p c u"),
             )
-            return grouped
+            return grouped[:]
 
-        v_codes = sb.tile([P, E], U32, name="v_codes", align_bytes=64)
-        v_scales = sb.tile([P, E], U8, name="v_scales", align_bytes=64)
-
-        def gather_values(c):
-            listed = sb.tile([P, I], BF16, name="val_listed%d" % c, align_bytes=64)
-            nc.vector.tensor_copy(listed[:], val_pool[c][:].indirect(offsets[:]))
-            return turn(listed, c, "v_g%d" % c)
-
-        def quantize_values(c, grouped):
-            cols = slice(c * P, (c + 1) * P)
-            nc.vector.quantize_mx(
-                out=v_codes[:, cols].bitcast(FP8X4), scales=v_scales[:, cols], in_=grouped[:].rearrange("p c t -> p (c t)")
+        offsets = sb.tile([P, I // 16], U16, name="offsets")
+        nc.sync.dma_start(offsets[:], offs)
+        val_pool0 = load_values(0)
+        scale_pool = tile([P, T], U8, "scale_pool")
+        nc.gpsimd.memset(scale_pool[:].bitcast(I32), 0)
+        for quad in range(4):
+            nc.sync.dma_start(
+                scale_pool[32 * quad : 32 * quad + 8, :].bitcast(I32),
+                krest_scales[:, 4 * quad : 4 * quad + 4, :].bitcast(I32),
             )
+        size_cols = tile([P, PACK], F32, "size_cols")
+        nc.sync.dma_start(size_cols[:], size.rearrange("o (p t) -> (o p) t", t=PACK))
+        word_pool = [tile([P, T], U32, "word_pool%d" % z) for z in range(2)]
+        for z in range(2):
+            nc.sync.dma_start(word_pool[z][:].bitcast(I32), krest_words[z].rearrange("p n t -> p (n t)").bitcast(I32))
+        query_raw = tile([P, PACK, Q], F32, "query_raw")
+        nc.sync.dma_start(query_raw[:], query.rearrange("(p t) q -> p t q", t=PACK))
 
-        v1 = gather_values(1)
-        inv_sum = sb.tile([P, 1], F32, name="inv_sum")
+        zeros = tile([P, P], F32, "zeros")
+        nc.gpsimd.memset(zeros[:], 0.0)
+        ident = tile([P, P], F32, "ident")
+        nc.gpsimd.affine_select(
+            out=ident[:], in_=zeros[:], compare_op=ALU.not_equal, fill=1.0, base=0, pattern=[[-1, P]], channel_multiplier=1
+        )
+
+        k_stage = tile([P, PACK * T], F32, "k_stage", "zeros")
+        k_rows = kfirst.rearrange("(p t) n -> p t n", t=PACK)
+        k_chunks = []
+        first = 0
+        for width in K_LOADS:
+            k_raw = k_stage[:, PACK * first : PACK * (first + width)].rearrange("p (t n) -> p t n", t=PACK)
+            nc.sync.dma_start(k_raw, k_rows[:, :, first : first + width])
+            k_chunks.extend(k_raw[:, :, lo : lo + CHUNK] for lo in range(0, width, CHUNK))
+            first = first + width
+
+        listed0 = gather_on_scalar(val_pool0, "listed0")
+        words_listed = [tile([P, I], U32, "words_listed%d" % z) for z in range(2)]
+        scale_listed = tile([P, I], U8, "scale_listed")
+        gather_on_vector(scale_listed, scale_pool)
+        for z in range(2):
+            gather_on_vector(words_listed[z], word_pool[z])
+
+        query_g = ring_tile([P, Q, PACK], "query_g")
+        interleave(nc.scalar.copy, query_g[:], query_raw[:])
+        query_mx = columns(mx_tiles(Q, "query"), 0, Q)
+        quantize(query_mx, query_g[:])
+
+        v0_mx = columns(mx_tiles(P, "v0"), 0, P)
+        quantize(v0_mx, turn(listed0, 7, "v0_g"))
+        size_rows = bank(7, [P, PACK, P])
+        for t in range(PACK):
+            nc.tensor.transpose(size_rows[:, t, :], size_cols[:, t : t + 1].to_broadcast([P, P]), ident[:])
+
+        val_pool1 = load_values(1, "listed0")
+        qrest_stage = tile([P, 2 * PACK * Q], F32, "qrest_stage", "v0_g")
+        qrest_raw = qrest_stage[:].rearrange("p (z t q) -> p z t q", z=2, t=PACK)
+        for z in range(2):
+            nc.sync.dma_start(qrest_raw[:, z], qrest[z * PASS : (z + 1) * PASS, :].rearrange("(p t) q -> p t q", t=PACK))
+        val_pool2 = load_values(2, "size_cols")
+
+        a_banks = [bank(0, [P, 2 * CHUNK]), bank(1, [P, CHUNK]), bank(2, [P, CHUNK])]
+        a_parts = [a_banks[0][:, :CHUNK], a_banks[0][:, CHUNK:], a_banks[1][:], a_banks[2][:]]
+        for c in range(T // CHUNK):
+            k_g = ring_tile([P, CHUNK, PACK], "k_g%d" % c)
+            share = VECTOR_SHARE[c]
+            interleave(nc.vector.tensor_copy, k_g[:, :share, :], k_chunks[c][:, :, :share])
+            interleave(nc.scalar.copy, k_g[:, share:, :], k_chunks[c][:, :, share:])
+            k_mx = columns(mx_tiles(CHUNK, "k%d" % c), 0, CHUNK)
+            quantize(k_mx, k_g[:])
+            product(a_parts[c], query_mx, k_mx)
+        val_pool3 = load_values(3, "k0_codes")
+
+        a_all = tile([P, T], F32, "a_all", "zeros")
+        nc.scalar.copy(a_all[:, : 2 * CHUNK], a_banks[0][:])
+        nc.scalar.copy(a_all[:, 2 * CHUNK : 3 * CHUNK], a_banks[1][:])
+
+        qrest_g0 = ring_tile([P, Q, PACK], "qrest_g0")
+        interleave(nc.scalar.copy, qrest_g0[:], qrest_raw[:, 0])
+        nc.scalar.copy(a_all[:, 3 * CHUNK :], a_banks[2][:])
+        listed1 = ring_tile([P, I], "listed1")
+        gather_on_vector(listed1, val_pool1)
+        qrest_g1 = tile([P, Q, PACK], BF16, "qrest_g1", "listed0")
+        interleave(nc.vector.tensor_copy, qrest_g1[:], qrest_raw[:, 1])
+        b_acc = bank(4, [P, I])
+        for z, qrest_g in enumerate((qrest_g0, qrest_g1)):
+            qrest_mx = columns(mx_tiles(Q, "qrest%d" % z), 0, Q)
+            quantize(qrest_mx, qrest_g[:])
+            product(b_acc[:], qrest_mx, (words_listed[z][:], scale_listed[4 * z : P, :]), z == 0, z == 1)
+
+        a_listed = tile([P, I], F32, "a_listed", "listed0")
+        gather_on_vector(a_listed, a_all)
+        listed2 = gather_on_scalar(val_pool2, "listed2", "k3_codes")
+
+        s = tile([P, I], F32, "s")
+        nc.vector.tensor_tensor(s[:], a_listed[:], b_acc[:], ALU.add)
+        neg_max = tile([P, 1], F32, "neg_max")
+        nc.vector.tensor_reduce(neg_max[:], s[:], AX.X, ALU.max, negate=True)
+        p = tile([P, I], F32, "p", "k3_codes")
+        row_sum = tile([P, 1], F32, "row_sum")
+        nc.scalar.activation(p[:], s[:], ACT.Exp, bias=neg_max[:], scale=1.0, accum_out=row_sum[:])
+
+        listed3 = tile([P, I], BF16, "listed3", "listed0")
+        gather_on_vector(listed3, val_pool3)
+        v1_g = turn(listed1, 3, "v1_g", "neg_max")
+        inv_sum = tile([P, 1], F32, "inv_sum")
         nc.vector.reciprocal(inv_sum[:], row_sum[:])
-        w = sb.tile([P, I], BF16, name="w", align_bytes=64)
+        w = tile([P, I], BF16, "w")
         nc.vector.scalar_tensor_tensor(
             w[:].rearrange("q (p t) -> q p t", t=PACK),
             p[:].rearrange("q (p t) -> q p t", t=PACK),
@@ -199,26 +206,27 @@ def tile_attend_prefixfeatures_kernel(tc, query, kfirst, qrest, krest_words, kre
             ALU.mult,
             ALU.mult,
         )
-        listed0 = sb.tile([P, I], BF16, name="val_listed0", tag="s", align_bytes=64)
-        nc.scalar.activation(listed0[:], val_half[:].indirect(offsets[:]), ACT.Copy)
-        w_g = turn(w, 4, "w_g")
-        v0 = turn(listed0, 0, "v_g0")
-        v2 = gather_values(2)
-        quantize_values(1, v1)
-        w_mx = quantize(w_g, Q, "w")
-        w_op = (w_mx[0][:], w_mx[1][:])
-        quantize_values(0, v0)
+        v2_g = turn(listed2, 0, "v2_g", "row_sum")
+        v3_g = turn(listed3, 1, "v3_g", "s")
+        w_g = turn(w, 2, "w_g")
 
-        def finish(n, lo, hi, engine_copy, name):
-            acc = bank(n, [P, hi - lo])
-            product(acc[:], w_op, (v_codes[:, lo:hi], v_scales[:, lo:hi]), True, True)
-            res = sb.tile([P, hi - lo], F32, name=name)
+        v1_mx = columns(mx_tiles(P, "v1", "inv_sum"), 0, P)
+        quantize(v1_mx, v1_g)
+        v23_tiles = mx_tiles(2 * P, "v23", "k3_codes")
+        quantize(columns(v23_tiles, 0, P), v2_g)
+        quantize(columns(v23_tiles, P, 2 * P), v3_g)
+        w_mx = columns(mx_tiles(Q, "w"), 0, Q)
+        quantize(w_mx, w_g)
+
+        halves = (
+            (5, nc.scalar.copy, (v0_mx, v1_mx)),
+            (6, nc.vector.tensor_copy, (columns(v23_tiles, 0, 2 * P),)),
+        )
+        for h, (n, engine_copy, operands) in enumerate(halves):
+            acc = bank(n, [P, E // 2])
+            width = E // 2 // len(operands)
+            for j, v_mx in enumerate(operands):
+                product(acc[:, j * width : (j + 1) * width], w_mx, v_mx)
+            res = tile([P, E // 2], F32, "res%d" % h)
             engine_copy(res[:], acc[:])
-            nc.sync.dma_start(out[:, lo:hi], res[:])
-
-        finish(5, 0, 2 * P, nc.scalar.copy, "res0")
-        v3 = gather_values(3)
-        quantize_values(2, v2)
-        finish(6, 2 * P, 3 * P, nc.scalar.copy, "res1")
-        quantize_values(3, v3)
-        finish(4, 3 * P, 4 * P, nc.scalar.copy, "res2")
+            nc.sync.dma_start(out[:, h * E // 2 : (h + 1) * E // 2], res[:])

from contextlib import ExitStack

import concourse.mybir as mybir

D, T, I, Q, E, K = 512, 1024, 512, 128, 512, 1024
FLOPS = 2 * Q * (D * T + K * I + I * E)

F32 = mybir.dt.float32
BF16 = mybir.dt.bfloat16
I32 = mybir.dt.int32
U32 = mybir.dt.uint32
U16 = mybir.dt.uint16
U8 = mybir.dt.uint8
FP8X4 = mybir.dt.float8_e4m3fn_x4
ALU = mybir.AluOpType
ACT = mybir.ActivationFunctionType
AX = mybir.AxisListType

P = 128
PACK = 4
PASS = P * PACK
CHUNK = 256
K_LOADS = (512, 256, 256)
VECTOR_SHARE = (160, 160, 64, 128)


def tile_attend_prefixfeatures_kernel(tc, query, kfirst, qrest, krest_words, krest_scales, size, vals, offs, out):
    nc = tc.nc
    with ExitStack() as ctx:
        sb = ctx.enter_context(tc.tile_pool(name="sb", bufs=1))
        ps = ctx.enter_context(tc.psum_pool(name="ps", bufs=1))

        def tile(shape, dtype, name, after=None):
            return sb.tile(shape, dtype, name=name, tag=after or name, align_bytes=64)

        def ring_tile(shape, name):
            return sb.tile(shape, BF16, name=name, tag="ring", bufs=2, align_bytes=64)

        def bank(n, shape):
            return ps.tile(shape, F32, name="bank%d" % n, tag="bank%d" % n)

        def interleave(engine_copy, grouped, raw):
            engine_copy(grouped.rearrange("p (c i) t -> p c t i", i=4), raw.rearrange("p t (c i) -> p c t i", i=4))

        def mx_tiles(width, name, after=None):
            return tile([P, width], U32, name + "_codes", after), tile([P, width], U8, name + "_scales")

        def columns(operand, lo, hi):
            return operand[0][:, lo:hi], operand[1][:, lo:hi]

        def quantize(operand, grouped):
            nc.vector.quantize_mx(
                out=operand[0].bitcast(FP8X4), scales=operand[1], in_=grouped.rearrange("p c t -> p (c t)")
            )

        def product(acc, stationary, moving, start=True, stop=True):
            nc.tensor.matmul_mx(
                out=acc,
                lhsT=stationary[0].bitcast(FP8X4),
                lhsT_scale=stationary[1],
                rhs=moving[0].bitcast(FP8X4),
                rhs_scale=moving[1],
                start=start,
                stop=stop,
            )

        def load_values(c, after=None):
            pool = tile([P, T], F32, "val_pool%d" % c, after)
            nc.sync.dma_start(pool[:], vals[c * P : (c + 1) * P, :])
            return pool

        def gather_on_scalar(pool, name, after=None):
            rounded = tile([P, T], BF16, name + "_rounded", after)
            nc.scalar.activation(rounded[:], pool[:], ACT.Copy)
            listed = tile([P, I], BF16, name)
            nc.scalar.activation(listed[:], rounded[:].indirect(offsets[:]), ACT.Copy)
            return listed

        def gather_on_vector(listed, pool):
            nc.vector.tensor_copy(listed[:], pool[:].indirect(offsets[:]))

        def turn(src, n, name, after=None):
            words = src[:].bitcast(F32)
            turned = bank(n, [P, 2, P])
            for u in range(2):
                nc.tensor.transpose(turned[:, u, :], words[:, u : I // 2 : 2], ident[:])
            grouped = tile([P, P, PACK], BF16, name, after)
            nc.scalar.copy(
                grouped[:].rearrange("p c t -> p (c t)").bitcast(F32).rearrange("p (c u) -> p c u", u=2),
                turned[:].rearrange("p u c -> p c u"),
            )
            return grouped[:]

        offsets = sb.tile([P, I // 16], U16, name="offsets")
        nc.sync.dma_start(offsets[:], offs)
        val_pool0 = load_values(0)
        scale_pool = tile([P, T], U8, "scale_pool")
        nc.gpsimd.memset(scale_pool[:].bitcast(I32), 0)
        for quad in range(4):
            nc.sync.dma_start(
                scale_pool[32 * quad : 32 * quad + 8, :].bitcast(I32),
                krest_scales[:, 4 * quad : 4 * quad + 4, :].bitcast(I32),
            )
        size_cols = tile([P, PACK], F32, "size_cols")
        nc.sync.dma_start(size_cols[:], size.rearrange("o (p t) -> (o p) t", t=PACK))
        word_pool = [tile([P, T], U32, "word_pool%d" % z) for z in range(2)]
        for z in range(2):
            nc.sync.dma_start(word_pool[z][:].bitcast(I32), krest_words[z].rearrange("p n t -> p (n t)").bitcast(I32))
        query_raw = tile([P, PACK, Q], F32, "query_raw")
        nc.sync.dma_start(query_raw[:], query.rearrange("(p t) q -> p t q", t=PACK))

        zeros = tile([P, P], F32, "zeros")
        nc.gpsimd.memset(zeros[:], 0.0)
        ident = tile([P, P], F32, "ident")
        nc.gpsimd.affine_select(
            out=ident[:], in_=zeros[:], compare_op=ALU.not_equal, fill=1.0, base=0, pattern=[[-1, P]], channel_multiplier=1
        )

        k_stage = tile([P, PACK * T], F32, "k_stage", "zeros")
        k_rows = kfirst.rearrange("(p t) n -> p t n", t=PACK)
        k_chunks = []
        first = 0
        for width in K_LOADS:
            k_raw = k_stage[:, PACK * first : PACK * (first + width)].rearrange("p (t n) -> p t n", t=PACK)
            nc.sync.dma_start(k_raw, k_rows[:, :, first : first + width])
            k_chunks.extend(k_raw[:, :, lo : lo + CHUNK] for lo in range(0, width, CHUNK))
            first = first + width

        listed0 = gather_on_scalar(val_pool0, "listed0")
        words_listed = [tile([P, I], U32, "words_listed%d" % z) for z in range(2)]
        scale_listed = tile([P, I], U8, "scale_listed")
        gather_on_vector(scale_listed, scale_pool)
        for z in range(2):
            gather_on_vector(words_listed[z], word_pool[z])

        query_g = ring_tile([P, Q, PACK], "query_g")
        interleave(nc.scalar.copy, query_g[:], query_raw[:])
        query_mx = columns(mx_tiles(Q, "query"), 0, Q)
        quantize(query_mx, query_g[:])

        v0_mx = columns(mx_tiles(P, "v0"), 0, P)
        quantize(v0_mx, turn(listed0, 7, "v0_g"))
        size_rows = bank(7, [P, PACK, P])
        for t in range(PACK):
            nc.tensor.transpose(size_rows[:, t, :], size_cols[:, t : t + 1].to_broadcast([P, P]), ident[:])

        val_pool1 = load_values(1, "listed0")
        qrest_stage = tile([P, 2 * PACK * Q], F32, "qrest_stage", "v0_g")
        qrest_raw = qrest_stage[:].rearrange("p (z t q) -> p z t q", z=2, t=PACK)
        for z in range(2):
            nc.sync.dma_start(qrest_raw[:, z], qrest[z * PASS : (z + 1) * PASS, :].rearrange("(p t) q -> p t q", t=PACK))
        val_pool2 = load_values(2, "size_cols")

        a_banks = [bank(0, [P, 2 * CHUNK]), bank(1, [P, CHUNK]), bank(2, [P, CHUNK])]
        a_parts = [a_banks[0][:, :CHUNK], a_banks[0][:, CHUNK:], a_banks[1][:], a_banks[2][:]]
        for c in range(T // CHUNK):
            k_g = ring_tile([P, CHUNK, PACK], "k_g%d" % c)
            share = VECTOR_SHARE[c]
            interleave(nc.vector.tensor_copy, k_g[:, :share, :], k_chunks[c][:, :, :share])
            interleave(nc.scalar.copy, k_g[:, share:, :], k_chunks[c][:, :, share:])
            k_mx = columns(mx_tiles(CHUNK, "k%d" % c), 0, CHUNK)
            quantize(k_mx, k_g[:])
            product(a_parts[c], query_mx, k_mx)
        val_pool3 = load_values(3, "k0_codes")

        a_all = tile([P, T], F32, "a_all", "zeros")
        nc.scalar.copy(a_all[:, : 2 * CHUNK], a_banks[0][:])
        nc.scalar.copy(a_all[:, 2 * CHUNK : 3 * CHUNK], a_banks[1][:])

        qrest_g0 = ring_tile([P, Q, PACK], "qrest_g0")
        interleave(nc.scalar.copy, qrest_g0[:], qrest_raw[:, 0])
        nc.scalar.copy(a_all[:, 3 * CHUNK :], a_banks[2][:])
        listed1 = ring_tile([P, I], "listed1")
        gather_on_vector(listed1, val_pool1)
        qrest_g1 = tile([P, Q, PACK], BF16, "qrest_g1", "listed0")
        interleave(nc.vector.tensor_copy, qrest_g1[:], qrest_raw[:, 1])
        b_acc = bank(4, [P, I])
        for z, qrest_g in enumerate((qrest_g0, qrest_g1)):
            qrest_mx = columns(mx_tiles(Q, "qrest%d" % z), 0, Q)
            quantize(qrest_mx, qrest_g[:])
            product(b_acc[:], qrest_mx, (words_listed[z][:], scale_listed[4 * z : P, :]), z == 0, z == 1)

        a_listed = tile([P, I], F32, "a_listed", "listed0")
        gather_on_vector(a_listed, a_all)
        listed2 = gather_on_scalar(val_pool2, "listed2", "k3_codes")

        s = tile([P, I], F32, "s")
        nc.vector.tensor_tensor(s[:], a_listed[:], b_acc[:], ALU.add)
        neg_max = tile([P, 1], F32, "neg_max")
        nc.vector.tensor_reduce(neg_max[:], s[:], AX.X, ALU.max, negate=True)
        p = tile([P, I], F32, "p", "k3_codes")
        row_sum = tile([P, 1], F32, "row_sum")
        nc.scalar.activation(p[:], s[:], ACT.Exp, bias=neg_max[:], scale=1.0, accum_out=row_sum[:])

        listed3 = tile([P, I], BF16, "listed3", "listed0")
        gather_on_vector(listed3, val_pool3)
        v1_g = turn(listed1, 3, "v1_g", "neg_max")
        inv_sum = tile([P, 1], F32, "inv_sum")
        nc.vector.reciprocal(inv_sum[:], row_sum[:])
        w = tile([P, I], BF16, "w")
        nc.vector.scalar_tensor_tensor(
            w[:].rearrange("q (p t) -> q p t", t=PACK),
            p[:].rearrange("q (p t) -> q p t", t=PACK),
            inv_sum[:],
            size_rows[:].rearrange("q t p -> q p t"),
            ALU.mult,
            ALU.mult,
        )
        v2_g = turn(listed2, 0, "v2_g", "row_sum")
        v3_g = turn(listed3, 1, "v3_g", "s")
        w_g = turn(w, 2, "w_g")

        v1_mx = columns(mx_tiles(P, "v1", "inv_sum"), 0, P)
        quantize(v1_mx, v1_g)
        v23_tiles = mx_tiles(2 * P, "v23", "k3_codes")
        quantize(columns(v23_tiles, 0, P), v2_g)
        quantize(columns(v23_tiles, P, 2 * P), v3_g)
        w_mx = columns(mx_tiles(Q, "w"), 0, Q)
        quantize(w_mx, w_g)

        halves = (
            (5, nc.scalar.copy, (v0_mx, v1_mx)),
            (6, nc.vector.tensor_copy, (columns(v23_tiles, 0, 2 * P),)),
        )
        for h, (n, engine_copy, operands) in enumerate(halves):
            acc = bank(n, [P, E // 2])
            width = E // 2 // len(operands)
            for j, v_mx in enumerate(operands):
                product(acc[:, j * width : (j + 1) * width], w_mx, v_mx)
            res = tile([P, E // 2], F32, "res%d" % h)
            engine_copy(res[:], acc[:])
            nc.sync.dma_start(out[:, h * E // 2 : (h + 1) * E // 2], res[:])
